import numpy as np
import ml_dtypes


def mxq(x, axis, fmt="e4m3"):
    dtype, down = {"e4m3": (ml_dtypes.float8_e4m3fn, 7), "e5m2": (ml_dtypes.float8_e5m2, 14)}[fmt]
    v = np.moveaxis(np.asarray(x, np.float32).astype(ml_dtypes.bfloat16).astype(np.float64), axis, -1)
    blocks = v.reshape(v.shape[:-1] + (-1, 32))
    amax = np.abs(blocks).max(-1, keepdims=True)
    byte = np.maximum(np.where(amax > 0, np.frexp(amax)[1] - 1 + 127, 0) - down, 1)
    scale = np.exp2(byte - 127.0)
    codes = (blocks / scale).astype(np.float32).astype(dtype).astype(np.float64)
    return np.moveaxis((codes * scale).reshape(v.shape), -1, axis)


WIDE = False


def mx_kscale(k):
    if not WIDE:
        return np.ones(k)
    levels = np.array([10, -10, 5, -5, 0])
    if k % 512:
        return np.exp2(np.random.permutation(np.resize(levels, k // 32))).repeat(32)
    a = np.empty((k // 512, 16))
    for p in range(k // 512):
        a[p, :8] = np.random.permutation(np.resize(levels, 8))
        for g in range(8):
            far = levels[np.abs(levels - a[p, g]) >= 10]
            a[p, g + 8] = far[np.random.randint(len(far))]
    return np.exp2(a.ravel()).repeat(32)


def f64(x):
    return np.asarray(x).astype(np.float64)


def striped(idx):
    return np.tile(idx.reshape(-1, 16).T, (8, 1)).astype(np.uint16)


def unstriped(offs):
    return offs[:16].T.reshape(-1).astype(np.int64)


E2M1 = np.array([0.0, 0.5, 1.0, 1.5, 2.0, 3.0, 4.0, 6.0, -0.0, -0.5, -1.0, -1.5, -2.0, -3.0, -4.0, -6.0])


def pack_weight(w, fmt):
    k, n = w.shape
    w = f64(np.asarray(w, np.float32).astype(ml_dtypes.bfloat16)).reshape(k // 32, 32, n)
    amax = np.abs(w).max(1)
    if fmt == "e4m3":
        byte = np.frexp(amax)[1] - 1 + 127 - 7
    else:
        mant, ex = np.frexp(amax / 6.0)
        byte = np.where(mant > 0.5, ex, ex - 1) + 127
    byte = np.clip(np.where(amax > 0, byte, 1), 1, 254)
    scaled = (w * np.exp2(127.0 - byte)[:, None, :]).reshape(k, n).astype(np.float32)
    by_word = np.ascontiguousarray(scaled.reshape(k // 512, 128, 4, n).transpose(0, 1, 3, 2))
    if fmt == "e4m3":
        words = by_word.astype(ml_dtypes.float8_e4m3fn).view(np.uint8)
    else:
        c = by_word.astype(ml_dtypes.float4_e2m1fn).view(np.uint8) & 0xF
        words = (c[..., 0::2] | (c[..., 1::2] << 4)).reshape(k // 512, 128, 2 * n)
    return np.ascontiguousarray(words), np.ascontiguousarray(byte.astype(np.uint8).reshape(k // 512, 16, n))


def unpack_weight(words, scales, fmt):
    g, _, n = scales.shape
    words = np.ascontiguousarray(words).reshape(g, 128, n, -1)
    if fmt == "e4m3":
        vals = words.view(ml_dtypes.float8_e4m3fn).astype(np.float64)
    else:
        nib = np.empty((g, 128, n, 4), np.uint8)
        nib[..., 0::2] = words & 0xF
        nib[..., 1::2] = words >> 4
        vals = E2M1[nib]
    vals = vals * np.repeat(np.exp2(scales.astype(np.float64) - 127.0), 8, axis=1)[..., None]
    return vals.transpose(0, 1, 3, 2).reshape(g * 512, n)


def gelu(v):
    return 0.5 * v * (1.0 + np.tanh(np.sqrt(2.0 / np.pi) * (v + 0.044715 * v**3)))


K, K1, K2, H, T, S, T3, S2, P = 1536, 1024, 512, 1024, 4096, 1024, 2048, 512, 512

def setup_inputs():
    n = np.random.standard_normal
    s = mx_kscale(K)[:, None]
    u = mx_kscale(H)[:, None]
    tab_words, tab_scales = pack_weight(n((K, T)) * s, "e4m3")
    tab2_words, tab2_scales = pack_weight(n((H, T3)) / np.sqrt(H) / u, "e4m3")
    w4_words, w4_scales = pack_weight(n((K1, H)) / np.sqrt(K) / s[:K1], "e2m1")
    w1 = (n((K2, H)) / np.sqrt(K) / s[K1:]).astype(np.float32)
    base = n((H, S)).astype(np.float32)
    gain = (np.exp(0.3 * n(H)) * u[:, 0]).astype(np.float32)
    fam = np.exp(0.4 * n(H)).astype(np.float32)
    teen = (n(H) * u[:, 0]).astype(np.float32)
    lim = (0.7 * n(S2)).astype(np.float32)
    return {"tab_words": tab_words, "tab_scales": tab_scales, "offs": striped(np.random.permutation(T)[:S]),
            "tab2_words": tab2_words, "tab2_scales": tab2_scales, "offs2": striped(np.random.permutation(T3)[:S2]),
            "pos1": striped(np.random.permutation(S)[:P]), "pos2": striped(np.random.permutation(S)[:P]),
            "w4_words": w4_words, "w4_scales": w4_scales, "w1": w1, "base": base, "gain": gain,
            "fam": fam, "teen": teen, "lim": lim}

def reference(tab_words, tab_scales, offs, tab2_words, tab2_scales, offs2, pos1, pos2,
              w4_words, w4_scales, w1, base, gain, fam, teen, lim):
    v = unpack_weight(tab_words, tab_scales, "e4m3")[:, unstriped(offs)]
    v2 = unpack_weight(tab2_words, tab2_scales, "e4m3")[:, unstriped(offs2)]
    w4 = unpack_weight(w4_words, w4_scales, "e2m1")
    w1q = mxq(f64(w1), 0, "e4m3")
    y = w4.T @ v[:K1] + w1q.T @ v[K1:]
    h = f64(gain)[:, None] * np.maximum(y, f64(base))
    x1 = mxq(f64(fam)[:, None] * h[:, unstriped(pos1)], 0, "e4m3")
    x2 = mxq(h[:, unstriped(pos2)] + f64(teen)[:, None], 0, "e4m3")
    e1 = v2.T @ x1
    e2 = v2.T @ x2
    return e1 * np.maximum(e2, f64(lim)[:, None])

@@ -1,0 +1,301 @@
+from contextlib import ExitStack
+
+import concourse.mybir as mybir
+
+K, K1, K2, H, T, S, T3, S2, NP = 1536, 1024, 512, 1024, 4096, 1024, 2048, 512, 512
+FLOPS = 2 * K * H * S + 2 * 2 * H * S2 * NP
+
+F32 = mybir.dt.float32
+BF16 = mybir.dt.bfloat16
+I32 = mybir.dt.int32
+U32 = mybir.dt.uint32
+U16 = mybir.dt.uint16
+U8 = mybir.dt.uint8
+FP8X4 = mybir.dt.float8_e4m3fn_x4
+FP4X4 = mybir.dt.float4_e2m1fn_x4
+ALU = mybir.AluOpType
+ACT = mybir.ActivationFunctionType
+
+P = 128
+BANK = 512
+
+
+def tile_list_ride_proposal_scores_kernel(
+    tc, tab_words, tab_scales, offs, tab2_words, tab2_scales, offs2, pos1, pos2,
+    w4_words, w4_scales, w1, base, gain, fam, teen, lim, out,
+):
+    nc = tc.nc
+    with ExitStack() as ctx:
+        lists = ctx.enter_context(tc.tile_pool(name="lists", bufs=1))
+        keep = ctx.enter_context(tc.tile_pool(name="keep", bufs=1))
+        ring = ctx.enter_context(tc.tile_pool(name="ring", bufs=1))
+        psum = ctx.enter_context(tc.psum_pool(name="psum", bufs=1))
+
+        def kept(name, shape, dtype):
+            return keep.tile(shape, dtype, name=name, align_bytes=64)
+
+        def rung(name, shape, dtype, tag, bufs):
+            return ring.tile(shape, dtype, name=name, tag=tag, bufs=bufs, align_bytes=64)
+
+        def bank(name, n):
+            return psum.tile([P, BANK], F32, name=name, tag="bank%d" % n)
+
+        def load_list(name, src):
+            t = lists.tile([P, src.shape[1]], U16, name=name)
+            nc.sync.dma_start(t[:], src)
+            return t
+
+        scale_win = kept("scale_win", [P, 3 * T], U8)
+        nc.vector.memset(scale_win[:].bitcast(I32), 0)
+        w4s_raw = kept("w4s_raw", [P, 2 * H], U8)
+        nc.vector.memset(w4s_raw[:].bitcast(I32), 0)
+        v_planes = kept("v_planes", [P, 3 * S], U8)
+        nc.vector.memset(v_planes[:].bitcast(I32), 0)
+        scale_win2 = kept("scale_win2", [P, T3], U8)
+        nc.vector.memset(scale_win2[:].bitcast(I32), 0)
+
+        offs_t = load_list("offs_t", offs)
+        w4_raw = kept("w4_raw", [P, 2 * 2 * H], U8)
+        nc.sync.dma_start(
+            w4_raw[:].bitcast(I32).rearrange("p (a c) -> p a c", a=2),
+            w4_words.bitcast(I32).rearrange("a p c -> p a c"),
+        )
+        w1_rows = w1.rearrange("(p j) c -> p j c", j=4)
+
+        def load_w1(b):
+            raw = rung("w1_raw%d" % b, [P, 4, 512], F32, "w1_raw", 1)
+            nc.sync.dma_start(raw[:], w1_rows[:, :, 512 * b : 512 * (b + 1)])
+            return raw
+
+        w1_raw0 = load_w1(0)
+        nc.sync.dma_start(
+            scale_win[:].bitcast(I32)[4:P:8, :].rearrange("q (a t) -> q a t", a=3),
+            tab_scales.bitcast(I32).rearrange("a q t -> q a t"),
+        )
+        for quad in range(4):
+            nc.sync.dma_start(
+                w4s_raw[:].bitcast(I32)[32 * quad : 32 * quad + 4, :].rearrange("r (a c) -> r a c", a=2),
+                w4_scales.bitcast(I32).rearrange("a q c -> q a c")[4 * quad : 4 * quad + 4],
+            )
+
+        def load_words(name, words, a, width):
+            t = rung(name, [P, width], I32, "table", 3)
+            nc.sync.dma_start(t[:], words[a].rearrange("p t i -> p (t i)").bitcast(I32))
+            return t
+
+        tab0 = load_words("tab0", tab_words, 0, T)
+        tab1 = load_words("tab1", tab_words, 1, T)
+
+        w4_dealt = kept("w4_dealt", [P, 2 * 2 * H], U8)
+        nc.vector.tensor_copy(
+            w4_dealt[:].bitcast(U16).rearrange("p (g t q) -> p g t q", g=4, t=4),
+            w4_raw[:].bitcast(U16).rearrange("p (g q t) -> p g t q", g=4, t=4),
+        )
+
+        v_scales = kept("v_scales", [P, 3 * S], U8)
+        for a in range(3):
+            nc.vector.tensor_copy(v_scales[:, S * a : S * (a + 1)], scale_win[:, T * a : T * (a + 1)].indirect(offs_t[:]))
+        for quad in range(4):
+            nc.sync.dma_start(
+                v_planes[:].bitcast(I32)[32 * quad : 32 * quad + 4, :],
+                v_scales[:].bitcast(I32)[32 * quad + 4 : 32 * quad + 32 : 8, :],
+            )
+        tab2_ = load_words("tab2_", tab_words, 2, T)
+
+        base_rows = base.rearrange("(b p t) n -> b t p n", b=2, t=4)
+
+        def load_base(s):
+            t = kept("base%d" % s, [P, S], F32)
+            nc.sync.dma_start(t[:], base_rows[s // 4, s % 4])
+            return t
+
+        def load_vec(name, vec):
+            t = kept(name, [P, 2, 4], F32)
+            nc.sync.dma_start(t[:], vec.rearrange("(b p t) -> p b t", b=2, t=4))
+            return t
+
+        base_t = [load_base(0)]
+        pos_t = [load_list("pos1_t", pos1), load_list("pos2_t", pos2)]
+        gain_t = load_vec("gain_t", gain)
+        fam_t = load_vec("fam_t", fam)
+        teen_t = load_vec("teen_t", teen)
+        base_t.append(load_base(1))
+
+        w1_codes = [kept("w1_codes%d" % b, [P, 512], U32) for b in range(2)]
+        w1_scales = [kept("w1_scales%d" % b, [P, 512], U8) for b in range(2)]
+
+        def weave_w1(b, raw):
+            grouped = rung("w1_bf%d" % b, [P, 2048], BF16, "w1_bf", 1)
+            nc.scalar.activation(
+                grouped[:].rearrange("p (t m j) -> p m j t", t=4, j=4),
+                raw[:].rearrange("p j (m t) -> p m j t", t=4),
+                ACT.Copy,
+            )
+            return grouped
+
+        def quantize_w1(b, grouped):
+            nc.vector.quantize_mx(w1_codes[b][:].bitcast(FP8X4), w1_scales[b][:], grouped[:])
+
+        w1_bf0 = weave_w1(0, w1_raw0)
+
+        w4s_dealt = kept("w4s_dealt", [P, 2 * H], U8)
+        nc.vector.tensor_copy(
+            w4s_dealt[:].rearrange("p (g t q) -> p g t q", g=4, t=4),
+            w4s_raw[:].rearrange("p (g q t) -> p g t q", g=4, t=4),
+        )
+        v_codes = [kept("v_codes%d" % a, [P, S], U32) for a in range(2)]
+        nc.vector.tensor_copy(v_codes[0][:], tab0[:].bitcast(U32).indirect(offs_t[:]))
+        quantize_w1(0, w1_bf0)
+        nc.vector.tensor_copy(v_codes[1][:], tab1[:].bitcast(U32).indirect(offs_t[:]))
+        v_last = [kept("v_last%d" % h, [P, BANK], U32) for h in range(2)]
+        for h in range(2):
+            nc.vector.tensor_copy(v_last[h][:], tab2_[:].bitcast(U32).indirect(offs_t[:, 32 * h : 32 * (h + 1)]))
+
+        w1_raw1 = load_w1(1)
+        base_t.append(load_base(2))
+        base_t.append(load_base(3))
+        offs2_t = load_list("offs2_t", offs2)
+        for quad in range(4):
+            nc.sync.dma_start(
+                scale_win2[:].bitcast(I32)[32 * quad : 32 * quad + 8, :],
+                tab2_scales.bitcast(I32)[:, 4 * quad : 4 * quad + 4, :],
+            )
+        rides = [load_words("rides%d" % a, tab2_words, a, T3) for a in range(2)]
+        for s in range(4, 8):
+            base_t.append(load_base(s))
+        lim_t = kept("lim_t", [P, 4], F32)
+        with nc.allow_non_contiguous_dma(reason="one value of lim for each partition"):
+            nc.sync.dma_start(lim_t[:], lim.rearrange("(i p) -> p i", p=P))
+
+        famgain = kept("famgain", [P, 2, 4], F32)
+        nc.vector.tensor_tensor(famgain[:], fam_t[:], gain_t[:], ALU.mult)
+
+        def first_pass(acc, s, h, a):
+            cols = slice(BANK * h, BANK * (h + 1))
+            plane = v_planes[:, S * a + BANK * h : S * a + BANK * (h + 1)]
+            if a < 2:
+                c0 = H * a + P * s
+                nc.tensor.matmul_mx(
+                    acc[:], lhsT=w4_dealt[:, 2 * c0 : 2 * (c0 + P)].bitcast(FP4X4), lhsT_scale=w4s_dealt[:, c0 : c0 + P],
+                    rhs=v_codes[a][:, cols].bitcast(FP8X4), rhs_scale=plane, start=(a == 0), stop=False,
+                )
+            else:
+                b, t = divmod(s, 4)
+                nc.tensor.matmul_mx(
+                    acc[:], lhsT=w1_codes[b][:, P * t : P * (t + 1)].bitcast(FP8X4), lhsT_scale=w1_scales[b][:, P * t : P * (t + 1)],
+                    rhs=v_last[h][:].bitcast(FP8X4), rhs_scale=plane, start=False, stop=True,
+                )
+
+        y = {}
+        for s in range(4):
+            for h in range(2):
+                y[s, h] = bank("y%d_%d" % (s, h), 2 * s + h)
+        for s in range(4):
+            for h in range(2):
+                first_pass(y[s, h], s, h, 0)
+        for s in range(2):
+            for h in range(2):
+                first_pass(y[s, h], s, h, 1)
+        for h in range(2):
+            for s in range(2):
+                first_pass(y[s, h], s, h, 2)
+        for s in range(2, 4):
+            for h in range(2):
+                for a in range(1, 3):
+                    first_pass(y[s, h], s, h, a)
+
+        def first_stage(s):
+            for h in range(2):
+                y[s, h] = bank("y%d_%d" % (s, h), 2 * (s % 4) + h)
+                for a in range(3):
+                    first_pass(y[s, h], s, h, a)
+
+        m = {}
+
+        def floor(s):
+            m[s] = rung("m%d" % s, [P, S], F32, "m", 3)
+            for h in range(2):
+                cols = slice(BANK * h, BANK * (h + 1))
+                nc.vector.tensor_tensor(m[s][:, cols], y[s, h][:], base_t[s][:, cols], ALU.max)
+
+        planes = [kept("planes%d" % l, [P, 4, NP], BF16) for l in range(2)]
+        x_bf = {(b, l): kept("x_bf%d_%d" % (b, l), [P, 4 * NP], BF16) for b in range(2) for l in range(2)}
+        x_codes = {(b, l): kept("x_codes%d_%d" % (b, l), [P, NP], U32) for b in range(2) for l in range(2)}
+        x_scales = {(b, l): kept("x_scales%d_%d" % (b, l), [P, NP], U8) for b in range(2) for l in range(2)}
+
+        def pick(s):
+            b, t = divmod(s, 4)
+            for l in range(2):
+                g = rung("g%d_%d" % (s, l), [P, NP], F32, "g", 4)
+                nc.vector.tensor_copy(g[:], m[s][:].indirect(pos_t[l][:]))
+                dst = planes[l][:, t, :] if b == 0 else x_bf[b, l][:].rearrange("p (j t) -> p t j", t=4)[:, t, :]
+                if l == 0:
+                    nc.scalar.activation(dst, g[:], ACT.Copy, scale=famgain[:, b, t : t + 1])
+                else:
+                    nc.scalar.activation(dst, g[:], ACT.Identity, scale=gain_t[:, b, t : t + 1], bias=teen_t[:, b, t : t + 1])
+
+        def weave_x(l):
+            nc.scalar.copy(
+                x_bf[0, l][:].rearrange("p (c i t) -> p c t i", i=4, t=4),
+                planes[l][:].rearrange("p t (c i) -> p c t i", i=4),
+            )
+
+        def quantize_x(b, l):
+            nc.vector.quantize_mx(x_codes[b, l][:].bitcast(FP8X4), x_scales[b, l][:], x_bf[b, l][:])
+
+        r_codes = [kept("r_codes%d" % a, [P, S2], U32) for a in range(2)]
+        r_scales = kept("r_scales", [P, S2], U8)
+
+        def second_pass(acc, i, b, l):
+            cols = slice(P * i, P * (i + 1))
+            nc.tensor.matmul_mx(
+                acc[:], lhsT=r_codes[b][:, cols].bitcast(FP8X4), lhsT_scale=r_scales[4 * b : P, cols],
+                rhs=x_codes[b, l][:].bitcast(FP8X4), rhs_scale=x_scales[b, l][:], start=(b == 0), stop=(b == 1),
+            )
+
+        floor(0)
+        w1_bf1 = weave_w1(1, w1_raw1)
+        floor(1)
+        pick(0)
+        floor(2)
+        pick(1)
+        quantize_w1(1, w1_bf1)
+        first_stage(4)
+        first_stage(5)
+        floor(3)
+        pick(2)
+        first_stage(6)
+        floor(4)
+        pick(3)
+        first_stage(7)
+        weave_x(0)
+        weave_x(1)
+        floor(5)
+        pick(4)
+        for a in range(2):
+            nc.vector.tensor_copy(r_codes[a][:], rides[a][:].bitcast(U32).indirect(offs2_t[:]))
+        nc.vector.tensor_copy(r_scales[:], scale_win2[:].indirect(offs2_t[:]))
+        floor(6)
+        pick(5)
+        quantize_x(0, 0)
+        e = {}
+        for i in range(4):
+            e[0, i] = bank("e0_%d" % i, i)
+            second_pass(e[0, i], i, 0, 0)
+        pick(6)
+        floor(7)
+        quantize_x(0, 1)
+        for i in range(4):
+            e[1, i] = bank("e1_%d" % i, 4 + i)
+            second_pass(e[1, i], i, 0, 1)
+        pick(7)
+        for l in range(2):
+            quantize_x(1, l)
+            for i in range(4):
+                second_pass(e[l, i], i, 1, l)
+        for i in range(4):
+            fam_score = kept("fam_score%d" % i, [P, NP], F32)
+            nc.scalar.copy(fam_score[:], e[0, i][:])
+            score = kept("score%d" % i, [P, NP], F32)
+            nc.vector.scalar_tensor_tensor(score[:], e[1, i][:], lim_t[:, i : i + 1], fam_score[:], ALU.max, ALU.mult)
+            nc.sync.dma_start(out[P * i : P * (i + 1), :], score[:])

@@ -29,6 +29,7 @@ def tile_list_ride_proposal_scores_kernel(
         lists = ctx.enter_context(tc.tile_pool(name="lists", bufs=1))
         keep = ctx.enter_context(tc.tile_pool(name="keep", bufs=1))
         ring = ctx.enter_context(tc.tile_pool(name="ring", bufs=1))
+        shared = ctx.enter_context(tc.tile_pool(name="shared", bufs=1))
         psum = ctx.enter_context(tc.psum_pool(name="psum", bufs=1))
 
         def kept(name, shape, dtype):
@@ -36,6 +37,9 @@ def tile_list_ride_proposal_scores_kernel(
 
         def rung(name, shape, dtype, tag, bufs):
             return ring.tile(shape, dtype, name=name, tag=tag, bufs=bufs, align_bytes=64)
+
+        def placed(name, shape, dtype, kib):
+            return shared.tile(shape, dtype, name=name, offset=1024 * kib, align_bytes=64)
 
         def bank(name, n):
             return psum.tile([P, BANK], F32, name=name, tag="bank%d" % n)
@@ -45,17 +49,17 @@ def tile_list_ride_proposal_scores_kernel(
             nc.sync.dma_start(t[:], src)
             return t
 
-        scale_win = kept("scale_win", [P, 3 * T], U8)
+        scale_win = placed("scale_win", [P, 2 * T], U8, 32)
         nc.vector.memset(scale_win[:].bitcast(I32), 0)
         w4s_raw = kept("w4s_raw", [P, 2 * H], U8)
         nc.vector.memset(w4s_raw[:].bitcast(I32), 0)
         v_planes = kept("v_planes", [P, 3 * S], U8)
-        nc.vector.memset(v_planes[:].bitcast(I32), 0)
+        nc.gpsimd.memset(v_planes[:].bitcast(I32), 0)
         scale_win2 = kept("scale_win2", [P, T3], U8)
-        nc.vector.memset(scale_win2[:].bitcast(I32), 0)
+        nc.gpsimd.memset(scale_win2[:].bitcast(I32), 0)
 
         offs_t = load_list("offs_t", offs)
-        w4_raw = kept("w4_raw", [P, 2 * 2 * H], U8)
+        w4_raw = placed("w4_raw", [P, 2 * 2 * H], U8, 14)
         nc.sync.dma_start(
             w4_raw[:].bitcast(I32).rearrange("p (a c) -> p a c", a=2),
             w4_words.bitcast(I32).rearrange("a p c -> p a c"),
@@ -63,63 +67,36 @@ def tile_list_ride_proposal_scores_kernel(
         w1_rows = w1.rearrange("(p j) c -> p j c", j=4)
 
         def load_w1(b):
-            raw = rung("w1_raw%d" % b, [P, 4, 512], F32, "w1_raw", 1)
+            raw = placed("w1_raw%d" % b, [P, 4, 512], F32, (40, 16)[b])
             nc.sync.dma_start(raw[:], w1_rows[:, :, 512 * b : 512 * (b + 1)])
             return raw
 
+        pos_t = [load_list("pos1_t", pos1), load_list("pos2_t", pos2)]
+        offs2_t = load_list("offs2_t", offs2)
         w1_raw0 = load_w1(0)
         nc.sync.dma_start(
-            scale_win[:].bitcast(I32)[4:P:8, :].rearrange("q (a t) -> q a t", a=3),
-            tab_scales.bitcast(I32).rearrange("a q t -> q a t"),
+            scale_win[:].bitcast(I32)[4:P:8, :].rearrange("q (a t) -> q a t", a=2),
+            tab_scales.bitcast(I32)[0:2].rearrange("a q t -> q a t"),
         )
+        nc.sync.dma_start(scale_win[:].bitcast(I32)[0:P:8, T // 4 :], tab_scales.bitcast(I32)[2])
         for quad in range(4):
             nc.sync.dma_start(
                 w4s_raw[:].bitcast(I32)[32 * quad : 32 * quad + 4, :].rearrange("r (a c) -> r a c", a=2),
                 w4_scales.bitcast(I32).rearrange("a q c -> q a c")[4 * quad : 4 * quad + 4],
             )
 
-        def load_words(name, words, a, width):
-            t = rung(name, [P, width], I32, "table", 3)
+        def load_words(name, words, a, width, kib):
+            t = placed(name, [P, width], I32, kib)
             nc.sync.dma_start(t[:], words[a].rearrange("p t i -> p (t i)").bitcast(I32))
             return t
-
-        tab0 = load_words("tab0", tab_words, 0, T)
-        tab1 = load_words("tab1", tab_words, 1, T)
 
         w4_dealt = kept("w4_dealt", [P, 2 * 2 * H], U8)
         nc.vector.tensor_copy(
             w4_dealt[:].bitcast(U16).rearrange("p (g t q) -> p g t q", g=4, t=4),
             w4_raw[:].bitcast(U16).rearrange("p (g q t) -> p g t q", g=4, t=4),
         )
-
-        v_scales = kept("v_scales", [P, 3 * S], U8)
-        for a in range(3):
-            nc.vector.tensor_copy(v_scales[:, S * a : S * (a + 1)], scale_win[:, T * a : T * (a + 1)].indirect(offs_t[:]))
-        for quad in range(4):
-            nc.sync.dma_start(
-                v_planes[:].bitcast(I32)[32 * quad : 32 * quad + 4, :],
-                v_scales[:].bitcast(I32)[32 * quad + 4 : 32 * quad + 32 : 8, :],
-            )
-        tab2_ = load_words("tab2_", tab_words, 2, T)
-
-        base_rows = base.rearrange("(b p t) n -> b t p n", b=2, t=4)
-
-        def load_base(s):
-            t = kept("base%d" % s, [P, S], F32)
-            nc.sync.dma_start(t[:], base_rows[s // 4, s % 4])
-            return t
-
-        def load_vec(name, vec):
-            t = kept(name, [P, 2, 4], F32)
-            nc.sync.dma_start(t[:], vec.rearrange("(b p t) -> p b t", b=2, t=4))
-            return t
-
-        base_t = [load_base(0)]
-        pos_t = [load_list("pos1_t", pos1), load_list("pos2_t", pos2)]
-        gain_t = load_vec("gain_t", gain)
-        fam_t = load_vec("fam_t", fam)
-        teen_t = load_vec("teen_t", teen)
-        base_t.append(load_base(1))
+        tab0 = load_words("tab0", tab_words, 0, T, 0)
+        tab1 = load_words("tab1", tab_words, 1, T, 16)
 
         w1_codes = [kept("w1_codes%d" % b, [P, 512], U32) for b in range(2)]
         w1_scales = [kept("w1_scales%d" % b, [P, 512], U8) for b in range(2)]
@@ -138,6 +115,43 @@ def tile_list_ride_proposal_scores_kernel(
 
         w1_bf0 = weave_w1(0, w1_raw0)
 
+        v_scales = kept("v_scales", [P, 2 * S], U8)
+        for a in range(2):
+            nc.vector.tensor_copy(v_scales[:, S * a : S * (a + 1)], scale_win[:, T * a : T * (a + 1)].indirect(offs_t[:]))
+        for quad in range(4):
+            nc.sync.dma_start(
+                v_planes[:].bitcast(I32)[32 * quad : 32 * quad + 4, : 2 * S // 4],
+                v_scales[:].bitcast(I32)[32 * quad + 4 : 32 * quad + 32 : 8, :],
+            )
+        tab2_ = load_words("tab2_", tab_words, 2, T, 32)
+        for quad in range(4):
+            nc.sync.dma_start(
+                v_planes[:].bitcast(I32)[32 * quad : 32 * quad + 4, 2 * S // 4 :],
+                v_scales[:].bitcast(I32)[32 * quad : 32 * quad + 32 : 8, S // 4 :],
+            )
+
+        base_rows = base.rearrange("(b p t) n -> b t p n", b=2, t=4)
+
+        def load_base(s):
+            t = placed("base%d" % s, [P, S], F32, 4 * (s % 4))
+            nc.sync.dma_start(t[:], base_rows[s // 4, s % 4])
+            return t
+
+        def load_vec(name, vec):
+            t = kept(name, [P, 2, 4], F32)
+            nc.gpsimd.dma_start(t[:], vec.rearrange("(b p t) -> p b t", b=2, t=4))
+            return t
+
+        for quad in range(4):
+            nc.gpsimd.dma_start(
+                scale_win2[:].bitcast(I32)[32 * quad : 32 * quad + 8, :],
+                tab2_scales.bitcast(I32)[:, 4 * quad : 4 * quad + 4, :],
+            )
+        gain_t = load_vec("gain_t", gain)
+        fam_t = load_vec("fam_t", fam)
+        teen_t = load_vec("teen_t", teen)
+
+
         w4s_dealt = kept("w4s_dealt", [P, 2 * H], U8)
         nc.vector.tensor_copy(
             w4s_dealt[:].rearrange("p (g t q) -> p g t q", g=4, t=4),
@@ -147,28 +161,21 @@ def tile_list_ride_proposal_scores_kernel(
         nc.vector.tensor_copy(v_codes[0][:], tab0[:].bitcast(U32).indirect(offs_t[:]))
         quantize_w1(0, w1_bf0)
         nc.vector.tensor_copy(v_codes[1][:], tab1[:].bitcast(U32).indirect(offs_t[:]))
+        r_scales = placed("r_scales", [P, S2], U8, 24)
+        nc.vector.tensor_copy(r_scales[:], scale_win2[:].indirect(offs2_t[:]))
         v_last = [kept("v_last%d" % h, [P, BANK], U32) for h in range(2)]
         for h in range(2):
             nc.vector.tensor_copy(v_last[h][:], tab2_[:].bitcast(U32).indirect(offs_t[:, 32 * h : 32 * (h + 1)]))
 
+        base_t = [load_base(s) for s in range(4)]
         w1_raw1 = load_w1(1)
-        base_t.append(load_base(2))
-        base_t.append(load_base(3))
-        offs2_t = load_list("offs2_t", offs2)
-        for quad in range(4):
-            nc.sync.dma_start(
-                scale_win2[:].bitcast(I32)[32 * quad : 32 * quad + 8, :],
-                tab2_scales.bitcast(I32)[:, 4 * quad : 4 * quad + 4, :],
-            )
-        rides = [load_words("rides%d" % a, tab2_words, a, T3) for a in range(2)]
-        for s in range(4, 8):
-            base_t.append(load_base(s))
+        rides = [load_words("rides%d" % a, tab2_words, a, T3, 32 + 8 * a) for a in range(2)]
         lim_t = kept("lim_t", [P, 4], F32)
         with nc.allow_non_contiguous_dma(reason="one value of lim for each partition"):
-            nc.sync.dma_start(lim_t[:], lim.rearrange("(i p) -> p i", p=P))
+            nc.gpsimd.dma_start(lim_t[:], lim.rearrange("(i p) -> p i", p=P))
 
         famgain = kept("famgain", [P, 2, 4], F32)
-        nc.vector.tensor_tensor(famgain[:], fam_t[:], gain_t[:], ALU.mult)
+        nc.gpsimd.tensor_tensor(famgain[:], fam_t[:], gain_t[:], ALU.mult)
 
         def first_pass(acc, s, h, a):
             cols = slice(BANK * h, BANK * (h + 1))
@@ -211,22 +218,32 @@ def tile_list_ride_proposal_scores_kernel(
                     first_pass(y[s, h], s, h, a)
 
         m = {}
+        gs = {}
 
         def floor(s):
             m[s] = rung("m%d" % s, [P, S], F32, "m", 3)
             for h in range(2):
                 cols = slice(BANK * h, BANK * (h + 1))
                 nc.vector.tensor_tensor(m[s][:, cols], y[s, h][:], base_t[s][:, cols], ALU.max)
+            if s < 4:
+                base_t.append(load_base(s + 4))
 
         planes = [kept("planes%d" % l, [P, 4, NP], BF16) for l in range(2)]
         x_bf = {(b, l): kept("x_bf%d_%d" % (b, l), [P, 4 * NP], BF16) for b in range(2) for l in range(2)}
-        x_codes = {(b, l): kept("x_codes%d_%d" % (b, l), [P, NP], U32) for b in range(2) for l in range(2)}
+        x_codes = {(1, l): kept("x_codes1_%d" % l, [P, NP], U32) for l in range(2)}
         x_scales = {(b, l): kept("x_scales%d_%d" % (b, l), [P, NP], U8) for b in range(2) for l in range(2)}
 
         def pick(s):
             b, t = divmod(s, 4)
+            if s >= 6:
+                shifted = rung("shifted%d" % s, [P, S], F32, "shifted", 2)
+                nc.scalar.activation(shifted[:], m[s][:], ACT.Identity, scale=gain_t[:, b, t : t + 1], bias=teen_t[:, b, t : t + 1])
             for l in range(2):
+                if s >= 6 and l == 1:
+                    nc.vector.tensor_copy(x_bf[b, l][:].rearrange("p (j t) -> p t j", t=4)[:, t, :], shifted[:].indirect(pos_t[l][:]))
+                    continue
                 g = rung("g%d_%d" % (s, l), [P, NP], F32, "g", 4)
+                gs[s, l] = g
                 nc.vector.tensor_copy(g[:], m[s][:].indirect(pos_t[l][:]))
                 dst = planes[l][:, t, :] if b == 0 else x_bf[b, l][:].rearrange("p (j t) -> p t j", t=4)[:, t, :]
                 if l == 0:
@@ -244,7 +261,6 @@ def tile_list_ride_proposal_scores_kernel(
             nc.vector.quantize_mx(x_codes[b, l][:].bitcast(FP8X4), x_scales[b, l][:], x_bf[b, l][:])
 
         r_codes = [kept("r_codes%d" % a, [P, S2], U32) for a in range(2)]
-        r_scales = kept("r_scales", [P, S2], U8)
 
         def second_pass(acc, i, b, l):
             cols = slice(P * i, P * (i + 1))
@@ -274,25 +290,22 @@ def tile_list_ride_proposal_scores_kernel(
         pick(4)
         for a in range(2):
             nc.vector.tensor_copy(r_codes[a][:], rides[a][:].bitcast(U32).indirect(offs2_t[:]))
-        nc.vector.tensor_copy(r_scales[:], scale_win2[:].indirect(offs2_t[:]))
         floor(6)
         pick(5)
-        quantize_x(0, 0)
-        e = {}
-        for i in range(4):
-            e[0, i] = bank("e0_%d" % i, i)
-            second_pass(e[0, i], i, 0, 0)
         pick(6)
         floor(7)
-        quantize_x(0, 1)
-        for i in range(4):
-            e[1, i] = bank("e1_%d" % i, 4 + i)
-            second_pass(e[1, i], i, 0, 1)
+        e = {}
+        for l in range(2):
+            x_codes[0, l] = placed("x_codes0_%d" % l, [P, NP], U32, 12 + 2 * l)
+            quantize_x(0, l)
+            for i in range(4):
+                e[l, i] = bank("e%d_%d" % (l, i), 4 * l + i)
+                second_pass(e[l, i], i, 0, l)
         pick(7)
         for l in range(2):
             quantize_x(1, l)
-            for i in range(4):
-                second_pass(e[l, i], i, 1, l)
+        for l, i in ((0, 0), (0, 1), (1, 0), (0, 2), (1, 1), (0, 3), (1, 2), (1, 3)):
+            second_pass(e[l, i], i, 1, l)
         for i in range(4):
             fam_score = kept("fam_score%d" % i, [P, NP], F32)
             nc.scalar.copy(fam_score[:], e[0, i][:])

@@ -18,6 +18,7 @@ ACT = mybir.ActivationFunctionType
 
 P = 128
 BANK = 512
+BASE_AT = (0, 4, 24, 29)
 
 
 def tile_list_ride_proposal_scores_kernel(
@@ -39,7 +40,7 @@ def tile_list_ride_proposal_scores_kernel(
             return ring.tile(shape, dtype, name=name, tag=tag, bufs=bufs, align_bytes=64)
 
         def placed(name, shape, dtype, kib):
-            return shared.tile(shape, dtype, name=name, offset=1024 * kib, align_bytes=64)
+            return shared.tile(shape, dtype, name=name, offset=int(1024 * kib), align_bytes=64)
 
         def bank(name, n):
             return psum.tile([P, BANK], F32, name=name, tag="bank%d" % n)
@@ -67,7 +68,7 @@ def tile_list_ride_proposal_scores_kernel(
         w1_rows = w1.rearrange("(p j) c -> p j c", j=4)
 
         def load_w1(b):
-            raw = placed("w1_raw%d" % b, [P, 4, 512], F32, (40, 16)[b])
+            raw = placed("w1_raw%d" % b, [P, 4, 512], F32, (50, 16)[b])
             nc.sync.dma_start(raw[:], w1_rows[:, :, 512 * b : 512 * (b + 1)])
             return raw
 
@@ -84,6 +85,7 @@ def tile_list_ride_proposal_scores_kernel(
                 w4s_raw[:].bitcast(I32)[32 * quad : 32 * quad + 4, :].rearrange("r (a c) -> r a c", a=2),
                 w4_scales.bitcast(I32).rearrange("a q c -> q a c")[4 * quad : 4 * quad + 4],
             )
+        nc.sync.dma_start(scale_win2[:].bitcast(I32)[2:P:4, :], tab2_scales.bitcast(I32).rearrange("a q t -> (a q) t"))
 
         def load_words(name, words, a, width, kib):
             t = placed(name, [P, width], I32, kib)
@@ -133,23 +135,14 @@ def tile_list_ride_proposal_scores_kernel(
         base_rows = base.rearrange("(b p t) n -> b t p n", b=2, t=4)
 
         def load_base(s):
-            t = placed("base%d" % s, [P, S], F32, 4 * (s % 4))
+            t = placed("base%d" % s, [P, S], F32, BASE_AT[s % 4])
             nc.sync.dma_start(t[:], base_rows[s // 4, s % 4])
             return t
 
-        def load_vec(name, vec):
-            t = kept(name, [P, 2, 4], F32)
-            nc.gpsimd.dma_start(t[:], vec.rearrange("(b p t) -> p b t", b=2, t=4))
+        def load_vec(name, vec, kib):
+            t = placed(name, [P, 2, 4], F32, kib)
+            nc.sync.dma_start(t[:], vec.rearrange("(b p t) -> p b t", b=2, t=4))
             return t
-
-        for quad in range(4):
-            nc.gpsimd.dma_start(
-                scale_win2[:].bitcast(I32)[32 * quad : 32 * quad + 8, :],
-                tab2_scales.bitcast(I32)[:, 4 * quad : 4 * quad + 4, :],
-            )
-        gain_t = load_vec("gain_t", gain)
-        fam_t = load_vec("fam_t", fam)
-        teen_t = load_vec("teen_t", teen)
 
 
         w4s_dealt = kept("w4s_dealt", [P, 2 * H], U8)
@@ -161,61 +154,58 @@ def tile_list_ride_proposal_scores_kernel(
         nc.vector.tensor_copy(v_codes[0][:], tab0[:].bitcast(U32).indirect(offs_t[:]))
         quantize_w1(0, w1_bf0)
         nc.vector.tensor_copy(v_codes[1][:], tab1[:].bitcast(U32).indirect(offs_t[:]))
-        r_scales = placed("r_scales", [P, S2], U8, 24)
+        r_scales = placed("r_scales", [P, S2], U8, 28)
         nc.vector.tensor_copy(r_scales[:], scale_win2[:].indirect(offs2_t[:]))
         v_last = [kept("v_last%d" % h, [P, BANK], U32) for h in range(2)]
         for h in range(2):
             nc.vector.tensor_copy(v_last[h][:], tab2_[:].bitcast(U32).indirect(offs_t[:, 32 * h : 32 * (h + 1)]))
 
-        base_t = [load_base(s) for s in range(4)]
+        base_t = [load_base(s) for s in range(2)]
         w1_raw1 = load_w1(1)
-        rides = [load_words("rides%d" % a, tab2_words, a, T3, 32 + 8 * a) for a in range(2)]
-        lim_t = kept("lim_t", [P, 4], F32)
-        with nc.allow_non_contiguous_dma(reason="one value of lim for each partition"):
-            nc.gpsimd.dma_start(lim_t[:], lim.rearrange("(i p) -> p i", p=P))
+        gain_t = load_vec("gain_t", gain, 28.5)
+        fam_t = load_vec("fam_t", fam, 28.625)
+        teen_t = load_vec("teen_t", teen, 28.75)
+        base_t.append(load_base(2))
+        base_t.append(load_base(3))
+        rides = [load_words("rides%d" % a, tab2_words, a, T3, 34 + 8 * a) for a in range(2)]
 
-        famgain = kept("famgain", [P, 2, 4], F32)
-        nc.gpsimd.tensor_tensor(famgain[:], fam_t[:], gain_t[:], ALU.mult)
 
-        def first_pass(acc, s, h, a):
+        def first_pass(acc, s, h, a, start, stop):
             cols = slice(BANK * h, BANK * (h + 1))
             plane = v_planes[:, S * a + BANK * h : S * a + BANK * (h + 1)]
             if a < 2:
                 c0 = H * a + P * s
                 nc.tensor.matmul_mx(
                     acc[:], lhsT=w4_dealt[:, 2 * c0 : 2 * (c0 + P)].bitcast(FP4X4), lhsT_scale=w4s_dealt[:, c0 : c0 + P],
-                    rhs=v_codes[a][:, cols].bitcast(FP8X4), rhs_scale=plane, start=(a == 0), stop=False,
+                    rhs=v_codes[a][:, cols].bitcast(FP8X4), rhs_scale=plane, start=start, stop=stop,
                 )
             else:
                 b, t = divmod(s, 4)
                 nc.tensor.matmul_mx(
                     acc[:], lhsT=w1_codes[b][:, P * t : P * (t + 1)].bitcast(FP8X4), lhsT_scale=w1_scales[b][:, P * t : P * (t + 1)],
-                    rhs=v_last[h][:].bitcast(FP8X4), rhs_scale=plane, start=False, stop=True,
+                    rhs=v_last[h][:].bitcast(FP8X4), rhs_scale=plane, start=start, stop=stop,
                 )
 
         y = {}
-        for s in range(4):
-            for h in range(2):
-                y[s, h] = bank("y%d_%d" % (s, h), 2 * s + h)
-        for s in range(4):
-            for h in range(2):
-                first_pass(y[s, h], s, h, 0)
         for s in range(2):
             for h in range(2):
-                first_pass(y[s, h], s, h, 1)
+                y[s, h] = bank("y%d_%d" % (s, h), 2 * s + h)
+        for a in range(2):
+            for s in range(2):
+                for h in range(2):
+                    first_pass(y[s, h], s, h, a, a == 0, False)
         for h in range(2):
             for s in range(2):
-                first_pass(y[s, h], s, h, 2)
-        for s in range(2, 4):
-            for h in range(2):
-                for a in range(1, 3):
-                    first_pass(y[s, h], s, h, a)
+                first_pass(y[s, h], s, h, 2, False, True)
 
         def first_stage(s):
             for h in range(2):
                 y[s, h] = bank("y%d_%d" % (s, h), 2 * (s % 4) + h)
-                for a in range(3):
-                    first_pass(y[s, h], s, h, a)
+                for a in (2, 0, 1):
+                    first_pass(y[s, h], s, h, a, a == 2, a == 1)
+
+        first_stage(2)
+        first_stage(3)
 
         m = {}
         gs = {}
@@ -228,10 +218,10 @@ def tile_list_ride_proposal_scores_kernel(
             if s < 4:
                 base_t.append(load_base(s + 4))
 
-        planes = [kept("planes%d" % l, [P, 4, NP], BF16) for l in range(2)]
+        planes = kept("planes", [P, 4, NP], BF16)
         x_bf = {(b, l): kept("x_bf%d_%d" % (b, l), [P, 4 * NP], BF16) for b in range(2) for l in range(2)}
-        x_codes = {(1, l): kept("x_codes1_%d" % l, [P, NP], U32) for l in range(2)}
-        x_scales = {(b, l): kept("x_scales%d_%d" % (b, l), [P, NP], U8) for b in range(2) for l in range(2)}
+        x_codes = {(b, l): kept("x_codes%d_%d" % (b, l), [P, NP], U32) for b in range(2) for l in range(2)}
+        x_scales = {(1, l): kept("x_scales1_%d" % l, [P, NP], U8) for l in range(2)}
 
         def pick(s):
             b, t = divmod(s, 4)
@@ -242,10 +232,10 @@ def tile_list_ride_proposal_scores_kernel(
                 if s >= 6 and l == 1:
                     nc.vector.tensor_copy(x_bf[b, l][:].rearrange("p (j t) -> p t j", t=4)[:, t, :], shifted[:].indirect(pos_t[l][:]))
                     continue
-                g = rung("g%d_%d" % (s, l), [P, NP], F32, "g", 4)
+                g = rung("g%d_%d" % (s, l), [P, NP], F32, "g", 6)
                 gs[s, l] = g
                 nc.vector.tensor_copy(g[:], m[s][:].indirect(pos_t[l][:]))
-                dst = planes[l][:, t, :] if b == 0 else x_bf[b, l][:].rearrange("p (j t) -> p t j", t=4)[:, t, :]
+                dst = planes[:, t, :] if (b, l) == (0, 0) else x_bf[b, l][:].rearrange("p (j t) -> p t j", t=4)[:, t, :]
                 if l == 0:
                     nc.scalar.activation(dst, g[:], ACT.Copy, scale=famgain[:, b, t : t + 1])
                 else:
@@ -254,7 +244,7 @@ def tile_list_ride_proposal_scores_kernel(
         def weave_x(l):
             nc.scalar.copy(
                 x_bf[0, l][:].rearrange("p (c i t) -> p c t i", i=4, t=4),
-                planes[l][:].rearrange("p t (c i) -> p c t i", i=4),
+                planes[:].rearrange("p t (c i) -> p c t i", i=4),
             )
 
         def quantize_x(b, l):
@@ -265,12 +255,16 @@ def tile_list_ride_proposal_scores_kernel(
         def second_pass(acc, i, b, l):
             cols = slice(P * i, P * (i + 1))
             nc.tensor.matmul_mx(
-                acc[:], lhsT=r_codes[b][:, cols].bitcast(FP8X4), lhsT_scale=r_scales[4 * b : P, cols],
+                acc[:], lhsT=r_codes[b][:, cols].bitcast(FP8X4), lhsT_scale=r_planes[:, S2 * b + P * i : S2 * b + P * (i + 1)],
                 rhs=x_codes[b, l][:].bitcast(FP8X4), rhs_scale=x_scales[b, l][:], start=(b == 0), stop=(b == 1),
             )
 
         floor(0)
         w1_bf1 = weave_w1(1, w1_raw1)
+        famgain = kept("famgain", [P, 2, 4], F32)
+        for s in range(8):
+            b, t = divmod(s, 4)
+            nc.scalar.activation(famgain[:, b, t : t + 1], fam_t[:, b, t : t + 1], ACT.Copy, scale=gain_t[:, b, t : t + 1])
         floor(1)
         pick(0)
         floor(2)
@@ -283,24 +277,39 @@ def tile_list_ride_proposal_scores_kernel(
         first_stage(6)
         floor(4)
         pick(3)
+        r_planes = placed("r_planes", [P, 2 * S2], U8, BASE_AT[0])
+        nc.vector.memset(r_planes[:].bitcast(I32), 0)
+        for a in range(2):
+            for quad in range(4):
+                first = 64 * a + 16 * quad + 2
+                nc.sync.dma_start(
+                    r_planes[:].bitcast(I32)[32 * quad : 32 * quad + 4, S2 // 4 * a : S2 // 4 * (a + 1)],
+                    r_scales[:].bitcast(I32)[first : first + 13 : 4, :],
+                )
+        lim_t = placed("lim_t", [P, 4], F32, BASE_AT[0] + 2)
+        with nc.allow_non_contiguous_dma(reason="one value of lim for each partition"):
+            nc.sync.dma_start(lim_t[:], lim.rearrange("(i p) -> p i", p=P))
         first_stage(7)
         weave_x(0)
-        weave_x(1)
         floor(5)
         pick(4)
         for a in range(2):
             nc.vector.tensor_copy(r_codes[a][:], rides[a][:].bitcast(U32).indirect(offs2_t[:]))
-        floor(6)
-        pick(5)
-        pick(6)
-        floor(7)
         e = {}
-        for l in range(2):
-            x_codes[0, l] = placed("x_codes0_%d" % l, [P, NP], U32, 12 + 2 * l)
+
+        def open_scores(l):
+            x_scales[0, l] = placed("x_scales0_%d" % l, [P, NP], U8, BASE_AT[3] + l)
             quantize_x(0, l)
             for i in range(4):
                 e[l, i] = bank("e%d_%d" % (l, i), 4 * l + i)
                 second_pass(e[l, i], i, 0, l)
+
+        floor(6)
+        pick(5)
+        pick(6)
+        floor(7)
+        open_scores(0)
+        open_scores(1)
         pick(7)
         for l in range(2):
             quantize_x(1, l)

@@ -18,7 +18,7 @@ ACT = mybir.ActivationFunctionType
 
 P = 128
 BANK = 512
-BASE_AT = (0, 4, 24, 29)
+BASE_AT = (0, 4, 26, 31)
 
 
 def tile_list_ride_proposal_scores_kernel(
@@ -50,25 +50,22 @@ def tile_list_ride_proposal_scores_kernel(
             nc.sync.dma_start(t[:], src)
             return t
 
-        scale_win = placed("scale_win", [P, 2 * T], U8, 32)
+        scale_win = placed("scale_win", [P, 2 * T], U8, 34)
         nc.vector.memset(scale_win[:].bitcast(I32), 0)
         w4s_raw = kept("w4s_raw", [P, 2 * H], U8)
         nc.vector.memset(w4s_raw[:].bitcast(I32), 0)
         v_planes = kept("v_planes", [P, 3 * S], U8)
         nc.gpsimd.memset(v_planes[:].bitcast(I32), 0)
-        scale_win2 = kept("scale_win2", [P, T3], U8)
-        nc.gpsimd.memset(scale_win2[:].bitcast(I32), 0)
 
         offs_t = load_list("offs_t", offs)
-        w4_raw = placed("w4_raw", [P, 2 * 2 * H], U8, 14)
-        nc.sync.dma_start(
-            w4_raw[:].bitcast(I32).rearrange("p (a c) -> p a c", a=2),
-            w4_words.bitcast(I32).rearrange("a p c -> p a c"),
-        )
+        w4_raw = []
+        for a in range(2):
+            w4_raw.append(placed("w4_raw%d" % a, [P, 2 * H], U8, (14, 17)[a]))
+            nc.sync.dma_start(w4_raw[a][:].bitcast(I32), w4_words.bitcast(I32)[a])
         w1_rows = w1.rearrange("(p j) c -> p j c", j=4)
 
         def load_w1(b):
-            raw = placed("w1_raw%d" % b, [P, 4, 512], F32, (50, 16)[b])
+            raw = placed("w1_raw%d" % b, [P, 4, 512], F32, (52, 18)[b])
             nc.sync.dma_start(raw[:], w1_rows[:, :, 512 * b : 512 * (b + 1)])
             return raw
 
@@ -85,7 +82,6 @@ def tile_list_ride_proposal_scores_kernel(
                 w4s_raw[:].bitcast(I32)[32 * quad : 32 * quad + 4, :].rearrange("r (a c) -> r a c", a=2),
                 w4_scales.bitcast(I32).rearrange("a q c -> q a c")[4 * quad : 4 * quad + 4],
             )
-        nc.sync.dma_start(scale_win2[:].bitcast(I32)[2:P:4, :], tab2_scales.bitcast(I32).rearrange("a q t -> (a q) t"))
 
         def load_words(name, words, a, width, kib):
             t = placed(name, [P, width], I32, kib)
@@ -93,12 +89,16 @@ def tile_list_ride_proposal_scores_kernel(
             return t
 
         w4_dealt = kept("w4_dealt", [P, 2 * 2 * H], U8)
-        nc.vector.tensor_copy(
-            w4_dealt[:].bitcast(U16).rearrange("p (g t q) -> p g t q", g=4, t=4),
-            w4_raw[:].bitcast(U16).rearrange("p (g q t) -> p g t q", g=4, t=4),
-        )
+        for a in range(2):
+            nc.vector.tensor_copy(
+                w4_dealt[:, 2 * H * a : 2 * H * (a + 1)].bitcast(U16).rearrange("p (b t q) -> p b t q", b=2, t=4),
+                w4_raw[a][:].bitcast(U16).rearrange("p (b q t) -> p b t q", b=2, t=4),
+            )
         tab0 = load_words("tab0", tab_words, 0, T, 0)
-        tab1 = load_words("tab1", tab_words, 1, T, 16)
+        tab1 = load_words("tab1", tab_words, 1, T, 18)
+        scale_win2 = placed("scale_win2", [P, T3], U8, 16)
+        nc.vector.memset(scale_win2[:].bitcast(I32), 0)
+        nc.sync.dma_start(scale_win2[:].bitcast(I32)[2:P:4, :], tab2_scales.bitcast(I32).rearrange("a q t -> (a q) t"))
 
         w1_codes = [kept("w1_codes%d" % b, [P, 512], U32) for b in range(2)]
         w1_scales = [kept("w1_scales%d" % b, [P, 512], U8) for b in range(2)]
@@ -125,7 +125,7 @@ def tile_list_ride_proposal_scores_kernel(
                 v_planes[:].bitcast(I32)[32 * quad : 32 * quad + 4, : 2 * S // 4],
                 v_scales[:].bitcast(I32)[32 * quad + 4 : 32 * quad + 32 : 8, :],
             )
-        tab2_ = load_words("tab2_", tab_words, 2, T, 32)
+        tab2_ = load_words("tab2_", tab_words, 2, T, 34)
         for quad in range(4):
             nc.sync.dma_start(
                 v_planes[:].bitcast(I32)[32 * quad : 32 * quad + 4, 2 * S // 4 :],
@@ -154,7 +154,7 @@ def tile_list_ride_proposal_scores_kernel(
         nc.vector.tensor_copy(v_codes[0][:], tab0[:].bitcast(U32).indirect(offs_t[:]))
         quantize_w1(0, w1_bf0)
         nc.vector.tensor_copy(v_codes[1][:], tab1[:].bitcast(U32).indirect(offs_t[:]))
-        r_scales = placed("r_scales", [P, S2], U8, 28)
+        r_scales = placed("r_scales", [P, S2], U8, 30)
         nc.vector.tensor_copy(r_scales[:], scale_win2[:].indirect(offs2_t[:]))
         v_last = [kept("v_last%d" % h, [P, BANK], U32) for h in range(2)]
         for h in range(2):
@@ -162,12 +162,12 @@ def tile_list_ride_proposal_scores_kernel(
 
         base_t = [load_base(s) for s in range(2)]
         w1_raw1 = load_w1(1)
-        gain_t = load_vec("gain_t", gain, 28.5)
-        fam_t = load_vec("fam_t", fam, 28.625)
-        teen_t = load_vec("teen_t", teen, 28.75)
+        gain_t = load_vec("gain_t", gain, 30.5)
+        fam_t = load_vec("fam_t", fam, 30.625)
+        teen_t = load_vec("teen_t", teen, 30.75)
         base_t.append(load_base(2))
         base_t.append(load_base(3))
-        rides = [load_words("rides%d" % a, tab2_words, a, T3, 34 + 8 * a) for a in range(2)]
+        rides = [load_words("rides%d" % a, tab2_words, a, T3, 36 + 8 * a) for a in range(2)]
 
 
         def first_pass(acc, s, h, a, start, stop):
@@ -215,31 +215,33 @@ def tile_list_ride_proposal_scores_kernel(
             for h in range(2):
                 cols = slice(BANK * h, BANK * (h + 1))
                 nc.vector.tensor_tensor(m[s][:, cols], y[s, h][:], base_t[s][:, cols], ALU.max)
-            if s < 4:
-                base_t.append(load_base(s + 4))
 
         planes = kept("planes", [P, 4, NP], BF16)
         x_bf = {(b, l): kept("x_bf%d_%d" % (b, l), [P, 4 * NP], BF16) for b in range(2) for l in range(2)}
         x_codes = {(b, l): kept("x_codes%d_%d" % (b, l), [P, NP], U32) for b in range(2) for l in range(2)}
         x_scales = {(1, l): kept("x_scales1_%d" % l, [P, NP], U8) for l in range(2)}
 
-        def pick(s):
+        def plane(b, l, t):
+            return x_bf[b, l][:].rearrange("p (j t) -> p t j", t=4)[:, t, :]
+
+        def pick_families(s):
             b, t = divmod(s, 4)
-            if s >= 6:
+            g = rung("g%d" % s, [P, NP], F32, "g", 3)
+            nc.vector.tensor_copy(g[:], m[s][:].indirect(pos_t[0][:]))
+            dst = planes[:, t, :] if b == 0 else plane(b, 0, t)
+            nc.scalar.activation(dst, g[:], ACT.Copy, scale=famgain[:, b, t : t + 1])
+
+        def pick_teens(s):
+            b, t = divmod(s, 4)
+            affine = dict(scale=gain_t[:, b, t : t + 1], bias=teen_t[:, b, t : t + 1])
+            if s < 6:
+                g = base_t[s + 1][:, :NP]
+                nc.vector.tensor_copy(g, m[s][:].indirect(pos_t[1][:]))
+                nc.scalar.activation(plane(b, 1, t), g, ACT.Identity, **affine)
+            else:
                 shifted = rung("shifted%d" % s, [P, S], F32, "shifted", 2)
-                nc.scalar.activation(shifted[:], m[s][:], ACT.Identity, scale=gain_t[:, b, t : t + 1], bias=teen_t[:, b, t : t + 1])
-            for l in range(2):
-                if s >= 6 and l == 1:
-                    nc.vector.tensor_copy(x_bf[b, l][:].rearrange("p (j t) -> p t j", t=4)[:, t, :], shifted[:].indirect(pos_t[l][:]))
-                    continue
-                g = rung("g%d_%d" % (s, l), [P, NP], F32, "g", 6)
-                gs[s, l] = g
-                nc.vector.tensor_copy(g[:], m[s][:].indirect(pos_t[l][:]))
-                dst = planes[:, t, :] if (b, l) == (0, 0) else x_bf[b, l][:].rearrange("p (j t) -> p t j", t=4)[:, t, :]
-                if l == 0:
-                    nc.scalar.activation(dst, g[:], ACT.Copy, scale=famgain[:, b, t : t + 1])
-                else:
-                    nc.scalar.activation(dst, g[:], ACT.Identity, scale=gain_t[:, b, t : t + 1], bias=teen_t[:, b, t : t + 1])
+                nc.scalar.activation(shifted[:], m[s][:], ACT.Identity, **affine)
+                nc.vector.tensor_copy(plane(b, 1, t), shifted[:].indirect(pos_t[1][:]))
 
         def weave_x(l):
             nc.scalar.copy(
@@ -265,19 +267,35 @@ def tile_list_ride_proposal_scores_kernel(
         for s in range(8):
             b, t = divmod(s, 4)
             nc.scalar.activation(famgain[:, b, t : t + 1], fam_t[:, b, t : t + 1], ACT.Copy, scale=gain_t[:, b, t : t + 1])
+        base_t.append(load_base(4))
+        pick_families(0)
         floor(1)
-        pick(0)
+        pick_teens(0)
+        base_t.append(load_base(5))
+        pick_families(1)
         floor(2)
-        pick(1)
+        pick_teens(1)
+        base_t.append(load_base(6))
+        pick_families(2)
         quantize_w1(1, w1_bf1)
         first_stage(4)
         first_stage(5)
         floor(3)
-        pick(2)
+        pick_teens(2)
+        base_t.append(load_base(7))
+        pick_families(3)
         first_stage(6)
+        first_stage(7)
+        weave_x(0)
         floor(4)
-        pick(3)
-        r_planes = placed("r_planes", [P, 2 * S2], U8, BASE_AT[0])
+        pick_teens(3)
+        pick_families(4)
+        floor(5)
+        pick_teens(4)
+        pick_families(5)
+        for a in range(2):
+            nc.vector.tensor_copy(r_codes[a][:], rides[a][:].bitcast(U32).indirect(offs2_t[:]))
+        r_planes = placed("r_planes", [P, 2 * S2], U8, 36)
         nc.vector.memset(r_planes[:].bitcast(I32), 0)
         for a in range(2):
             for quad in range(4):
@@ -286,15 +304,9 @@ def tile_list_ride_proposal_scores_kernel(
                     r_planes[:].bitcast(I32)[32 * quad : 32 * quad + 4, S2 // 4 * a : S2 // 4 * (a + 1)],
                     r_scales[:].bitcast(I32)[first : first + 13 : 4, :],
                 )
-        lim_t = placed("lim_t", [P, 4], F32, BASE_AT[0] + 2)
+        lim_t = placed("lim_t", [P, 4], F32, 38)
         with nc.allow_non_contiguous_dma(reason="one value of lim for each partition"):
             nc.sync.dma_start(lim_t[:], lim.rearrange("(i p) -> p i", p=P))
-        first_stage(7)
-        weave_x(0)
-        floor(5)
-        pick(4)
-        for a in range(2):
-            nc.vector.tensor_copy(r_codes[a][:], rides[a][:].bitcast(U32).indirect(offs2_t[:]))
         e = {}
 
         def open_scores(l):
@@ -305,12 +317,14 @@ def tile_list_ride_proposal_scores_kernel(
                 second_pass(e[l, i], i, 0, l)
 
         floor(6)
-        pick(5)
-        pick(6)
+        pick_teens(5)
+        pick_families(6)
         floor(7)
+        pick_teens(6)
+        pick_families(7)
         open_scores(0)
         open_scores(1)
-        pick(7)
+        pick_teens(7)
         for l in range(2):
             quantize_x(1, l)
         for l, i in ((0, 0), (0, 1), (1, 0), (0, 2), (1, 1), (0, 3), (1, 2), (1, 3)):

from contextlib import ExitStack

import concourse.mybir as mybir

K, K1, K2, H, T, S, T3, S2, NP = 1536, 1024, 512, 1024, 4096, 1024, 2048, 512, 512
FLOPS = 2 * K * H * S + 2 * 2 * H * S2 * NP

F32 = mybir.dt.float32
BF16 = mybir.dt.bfloat16
I32 = mybir.dt.int32
U32 = mybir.dt.uint32
U16 = mybir.dt.uint16
U8 = mybir.dt.uint8
FP8X4 = mybir.dt.float8_e4m3fn_x4
FP4X4 = mybir.dt.float4_e2m1fn_x4
ALU = mybir.AluOpType
ACT = mybir.ActivationFunctionType

P = 128
BANK = 512
BASE_AT = (0, 4, 26, 31)


def tile_list_ride_proposal_scores_kernel(
    tc, tab_words, tab_scales, offs, tab2_words, tab2_scales, offs2, pos1, pos2,
    w4_words, w4_scales, w1, base, gain, fam, teen, lim, out,
):
    nc = tc.nc
    with ExitStack() as ctx:
        lists = ctx.enter_context(tc.tile_pool(name="lists", bufs=1))
        keep = ctx.enter_context(tc.tile_pool(name="keep", bufs=1))
        ring = ctx.enter_context(tc.tile_pool(name="ring", bufs=1))
        shared = ctx.enter_context(tc.tile_pool(name="shared", bufs=1))
        psum = ctx.enter_context(tc.psum_pool(name="psum", bufs=1))

        def kept(name, shape, dtype):
            return keep.tile(shape, dtype, name=name, align_bytes=64)

        def rung(name, shape, dtype, tag, bufs):
            return ring.tile(shape, dtype, name=name, tag=tag, bufs=bufs, align_bytes=64)

        def placed(name, shape, dtype, kib):
            return shared.tile(shape, dtype, name=name, offset=int(1024 * kib), align_bytes=64)

        def bank(name, n):
            return psum.tile([P, BANK], F32, name=name, tag="bank%d" % n)

        def load_list(name, src):
            t = lists.tile([P, src.shape[1]], U16, name=name)
            nc.sync.dma_start(t[:], src)
            return t

        scale_win = placed("scale_win", [P, 2 * T], U8, 34)
        nc.vector.memset(scale_win[:].bitcast(I32), 0)
        w4s_raw = kept("w4s_raw", [P, 2 * H], U8)
        nc.vector.memset(w4s_raw[:].bitcast(I32), 0)
        v_planes = kept("v_planes", [P, 3 * S], U8)
        nc.gpsimd.memset(v_planes[:].bitcast(I32), 0)

        offs_t = load_list("offs_t", offs)
        w4_raw = []
        for a in range(2):
            w4_raw.append(placed("w4_raw%d" % a, [P, 2 * H], U8, (14, 17)[a]))
            nc.sync.dma_start(w4_raw[a][:].bitcast(I32), w4_words.bitcast(I32)[a])
        w1_rows = w1.rearrange("(p j) c -> p j c", j=4)

        def load_w1(b):
            raw = placed("w1_raw%d" % b, [P, 4, 512], F32, (52, 18)[b])
            nc.sync.dma_start(raw[:], w1_rows[:, :, 512 * b : 512 * (b + 1)])
            return raw

        pos_t = [load_list("pos1_t", pos1), load_list("pos2_t", pos2)]
        offs2_t = load_list("offs2_t", offs2)
        w1_raw0 = load_w1(0)
        nc.sync.dma_start(
            scale_win[:].bitcast(I32)[4:P:8, :].rearrange("q (a t) -> q a t", a=2),
            tab_scales.bitcast(I32)[0:2].rearrange("a q t -> q a t"),
        )
        nc.sync.dma_start(scale_win[:].bitcast(I32)[0:P:8, T // 4 :], tab_scales.bitcast(I32)[2])
        for quad in range(4):
            nc.sync.dma_start(
                w4s_raw[:].bitcast(I32)[32 * quad : 32 * quad + 4, :].rearrange("r (a c) -> r a c", a=2),
                w4_scales.bitcast(I32).rearrange("a q c -> q a c")[4 * quad : 4 * quad + 4],
            )

        def load_words(name, words, a, width, kib):
            t = placed(name, [P, width], I32, kib)
            nc.sync.dma_start(t[:], words[a].rearrange("p t i -> p (t i)").bitcast(I32))
            return t

        w4_dealt = kept("w4_dealt", [P, 2 * 2 * H], U8)
        for a in range(2):
            nc.vector.tensor_copy(
                w4_dealt[:, 2 * H * a : 2 * H * (a + 1)].bitcast(U16).rearrange("p (b t q) -> p b t q", b=2, t=4),
                w4_raw[a][:].bitcast(U16).rearrange("p (b q t) -> p b t q", b=2, t=4),
            )
        tab0 = load_words("tab0", tab_words, 0, T, 0)
        tab1 = load_words("tab1", tab_words, 1, T, 18)
        scale_win2 = placed("scale_win2", [P, T3], U8, 16)
        nc.vector.memset(scale_win2[:].bitcast(I32), 0)
        nc.sync.dma_start(scale_win2[:].bitcast(I32)[2:P:4, :], tab2_scales.bitcast(I32).rearrange("a q t -> (a q) t"))

        w1_codes = [kept("w1_codes%d" % b, [P, 512], U32) for b in range(2)]
        w1_scales = [kept("w1_scales%d" % b, [P, 512], U8) for b in range(2)]

        def weave_w1(b, raw):
            grouped = rung("w1_bf%d" % b, [P, 2048], BF16, "w1_bf", 1)
            nc.scalar.activation(
                grouped[:].rearrange("p (t m j) -> p m j t", t=4, j=4),
                raw[:].rearrange("p j (m t) -> p m j t", t=4),
                ACT.Copy,
            )
            return grouped

        def quantize_w1(b, grouped):
            nc.vector.quantize_mx(w1_codes[b][:].bitcast(FP8X4), w1_scales[b][:], grouped[:])

        w1_bf0 = weave_w1(0, w1_raw0)

        v_scales = kept("v_scales", [P, 2 * S], U8)
        for a in range(2):
            nc.vector.tensor_copy(v_scales[:, S * a : S * (a + 1)], scale_win[:, T * a : T * (a + 1)].indirect(offs_t[:]))
        for quad in range(4):
            nc.sync.dma_start(
                v_planes[:].bitcast(I32)[32 * quad : 32 * quad + 4, : 2 * S // 4],
                v_scales[:].bitcast(I32)[32 * quad + 4 : 32 * quad + 32 : 8, :],
            )
        tab2_ = load_words("tab2_", tab_words, 2, T, 34)
        for quad in range(4):
            nc.sync.dma_start(
                v_planes[:].bitcast(I32)[32 * quad : 32 * quad + 4, 2 * S // 4 :],
                v_scales[:].bitcast(I32)[32 * quad : 32 * quad + 32 : 8, S // 4 :],
            )

        base_rows = base.rearrange("(b p t) n -> b t p n", b=2, t=4)

        def load_base(s):
            t = placed("base%d" % s, [P, S], F32, BASE_AT[s % 4])
            nc.sync.dma_start(t[:], base_rows[s // 4, s % 4])
            return t

        def load_vec(name, vec, kib):
            t = placed(name, [P, 2, 4], F32, kib)
            nc.sync.dma_start(t[:], vec.rearrange("(b p t) -> p b t", b=2, t=4))
            return t


        w4s_dealt = kept("w4s_dealt", [P, 2 * H], U8)
        nc.vector.tensor_copy(
            w4s_dealt[:].rearrange("p (g t q) -> p g t q", g=4, t=4),
            w4s_raw[:].rearrange("p (g q t) -> p g t q", g=4, t=4),
        )
        v_codes = [kept("v_codes%d" % a, [P, S], U32) for a in range(2)]
        nc.vector.tensor_copy(v_codes[0][:], tab0[:].bitcast(U32).indirect(offs_t[:]))
        quantize_w1(0, w1_bf0)
        nc.vector.tensor_copy(v_codes[1][:], tab1[:].bitcast(U32).indirect(offs_t[:]))
        r_scales = placed("r_scales", [P, S2], U8, 30)
        nc.vector.tensor_copy(r_scales[:], scale_win2[:].indirect(offs2_t[:]))
        v_last = [kept("v_last%d" % h, [P, BANK], U32) for h in range(2)]
        for h in range(2):
            nc.vector.tensor_copy(v_last[h][:], tab2_[:].bitcast(U32).indirect(offs_t[:, 32 * h : 32 * (h + 1)]))

        base_t = [load_base(s) for s in range(2)]
        w1_raw1 = load_w1(1)
        gain_t = load_vec("gain_t", gain, 30.5)
        fam_t = load_vec("fam_t", fam, 30.625)
        teen_t = load_vec("teen_t", teen, 30.75)
        base_t.append(load_base(2))
        base_t.append(load_base(3))
        rides = [load_words("rides%d" % a, tab2_words, a, T3, 36 + 8 * a) for a in range(2)]


        def first_pass(acc, s, h, a, start, stop):
            cols = slice(BANK * h, BANK * (h + 1))
            plane = v_planes[:, S * a + BANK * h : S * a + BANK * (h + 1)]
            if a < 2:
                c0 = H * a + P * s
                nc.tensor.matmul_mx(
                    acc[:], lhsT=w4_dealt[:, 2 * c0 : 2 * (c0 + P)].bitcast(FP4X4), lhsT_scale=w4s_dealt[:, c0 : c0 + P],
                    rhs=v_codes[a][:, cols].bitcast(FP8X4), rhs_scale=plane, start=start, stop=stop,
                )
            else:
                b, t = divmod(s, 4)
                nc.tensor.matmul_mx(
                    acc[:], lhsT=w1_codes[b][:, P * t : P * (t + 1)].bitcast(FP8X4), lhsT_scale=w1_scales[b][:, P * t : P * (t + 1)],
                    rhs=v_last[h][:].bitcast(FP8X4), rhs_scale=plane, start=start, stop=stop,
                )

        y = {}
        for s in range(2):
            for h in range(2):
                y[s, h] = bank("y%d_%d" % (s, h), 2 * s + h)
        for a in range(2):
            for s in range(2):
                for h in range(2):
                    first_pass(y[s, h], s, h, a, a == 0, False)
        for h in range(2):
            for s in range(2):
                first_pass(y[s, h], s, h, 2, False, True)

        def first_stage(s):
            for h in range(2):
                y[s, h] = bank("y%d_%d" % (s, h), 2 * (s % 4) + h)
                for a in (2, 0, 1):
                    first_pass(y[s, h], s, h, a, a == 2, a == 1)

        first_stage(2)
        first_stage(3)

        m = {}
        gs = {}

        def floor(s):
            m[s] = rung("m%d" % s, [P, S], F32, "m", 3)
            for h in range(2):
                cols = slice(BANK * h, BANK * (h + 1))
                nc.vector.tensor_tensor(m[s][:, cols], y[s, h][:], base_t[s][:, cols], ALU.max)

        planes = kept("planes", [P, 4, NP], BF16)
        x_bf = {(b, l): kept("x_bf%d_%d" % (b, l), [P, 4 * NP], BF16) for b in range(2) for l in range(2)}
        x_codes = {(b, l): kept("x_codes%d_%d" % (b, l), [P, NP], U32) for b in range(2) for l in range(2)}
        x_scales = {(1, l): kept("x_scales1_%d" % l, [P, NP], U8) for l in range(2)}

        def plane(b, l, t):
            return x_bf[b, l][:].rearrange("p (j t) -> p t j", t=4)[:, t, :]

        def pick_families(s):
            b, t = divmod(s, 4)
            g = rung("g%d" % s, [P, NP], F32, "g", 3)
            nc.vector.tensor_copy(g[:], m[s][:].indirect(pos_t[0][:]))
            dst = planes[:, t, :] if b == 0 else plane(b, 0, t)
            nc.scalar.activation(dst, g[:], ACT.Copy, scale=famgain[:, b, t : t + 1])

        def pick_teens(s):
            b, t = divmod(s, 4)
            affine = dict(scale=gain_t[:, b, t : t + 1], bias=teen_t[:, b, t : t + 1])
            if s < 6:
                g = base_t[s + 1][:, :NP]
                nc.vector.tensor_copy(g, m[s][:].indirect(pos_t[1][:]))
                nc.scalar.activation(plane(b, 1, t), g, ACT.Identity, **affine)
            else:
                shifted = rung("shifted%d" % s, [P, S], F32, "shifted", 2)
                nc.scalar.activation(shifted[:], m[s][:], ACT.Identity, **affine)
                nc.vector.tensor_copy(plane(b, 1, t), shifted[:].indirect(pos_t[1][:]))

        def weave_x(l):
            nc.scalar.copy(
                x_bf[0, l][:].rearrange("p (c i t) -> p c t i", i=4, t=4),
                planes[:].rearrange("p t (c i) -> p c t i", i=4),
            )

        def quantize_x(b, l):
            nc.vector.quantize_mx(x_codes[b, l][:].bitcast(FP8X4), x_scales[b, l][:], x_bf[b, l][:])

        r_codes = [kept("r_codes%d" % a, [P, S2], U32) for a in range(2)]

        def second_pass(acc, i, b, l):
            cols = slice(P * i, P * (i + 1))
            nc.tensor.matmul_mx(
                acc[:], lhsT=r_codes[b][:, cols].bitcast(FP8X4), lhsT_scale=r_planes[:, S2 * b + P * i : S2 * b + P * (i + 1)],
                rhs=x_codes[b, l][:].bitcast(FP8X4), rhs_scale=x_scales[b, l][:], start=(b == 0), stop=(b == 1),
            )

        floor(0)
        w1_bf1 = weave_w1(1, w1_raw1)
        famgain = kept("famgain", [P, 2, 4], F32)
        for s in range(8):
            b, t = divmod(s, 4)
            nc.scalar.activation(famgain[:, b, t : t + 1], fam_t[:, b, t : t + 1], ACT.Copy, scale=gain_t[:, b, t : t + 1])
        base_t.append(load_base(4))
        pick_families(0)
        floor(1)
        pick_teens(0)
        base_t.append(load_base(5))
        pick_families(1)
        floor(2)
        pick_teens(1)
        base_t.append(load_base(6))
        pick_families(2)
        quantize_w1(1, w1_bf1)
        first_stage(4)
        first_stage(5)
        floor(3)
        pick_teens(2)
        base_t.append(load_base(7))
        pick_families(3)
        first_stage(6)
        first_stage(7)
        weave_x(0)
        floor(4)
        pick_teens(3)
        pick_families(4)
        floor(5)
        pick_teens(4)
        pick_families(5)
        for a in range(2):
            nc.vector.tensor_copy(r_codes[a][:], rides[a][:].bitcast(U32).indirect(offs2_t[:]))
        r_planes = placed("r_planes", [P, 2 * S2], U8, 36)
        nc.vector.memset(r_planes[:].bitcast(I32), 0)
        for a in range(2):
            for quad in range(4):
                first = 64 * a + 16 * quad + 2
                nc.sync.dma_start(
                    r_planes[:].bitcast(I32)[32 * quad : 32 * quad + 4, S2 // 4 * a : S2 // 4 * (a + 1)],
                    r_scales[:].bitcast(I32)[first : first + 13 : 4, :],
                )
        lim_t = placed("lim_t", [P, 4], F32, 38)
        with nc.allow_non_contiguous_dma(reason="one value of lim for each partition"):
            nc.sync.dma_start(lim_t[:], lim.rearrange("(i p) -> p i", p=P))
        e = {}

        def open_scores(l):
            x_scales[0, l] = placed("x_scales0_%d" % l, [P, NP], U8, BASE_AT[3] + l)
            quantize_x(0, l)
            for i in range(4):
                e[l, i] = bank("e%d_%d" % (l, i), 4 * l + i)
                second_pass(e[l, i], i, 0, l)

        floor(6)
        pick_teens(5)
        pick_families(6)
        floor(7)
        pick_teens(6)
        pick_families(7)
        open_scores(0)
        open_scores(1)
        pick_teens(7)
        for l in range(2):
            quantize_x(1, l)
        for l, i in ((0, 0), (0, 1), (1, 0), (0, 2), (1, 1), (0, 3), (1, 2), (1, 3)):
            second_pass(e[l, i], i, 1, l)
        for i in range(4):
            fam_score = kept("fam_score%d" % i, [P, NP], F32)
            nc.scalar.copy(fam_score[:], e[0, i][:])
            score = kept("score%d" % i, [P, NP], F32)
            nc.vector.scalar_tensor_tensor(score[:], e[1, i][:], lim_t[:, i : i + 1], fam_score[:], ALU.max, ALU.mult)
            nc.sync.dma_start(out[P * i : P * (i + 1), :], score[:])
